import numpy as np
import ml_dtypes


def mxq(x, axis, fmt="e4m3"):
    dtype, down = {"e4m3": (ml_dtypes.float8_e4m3fn, 7), "e5m2": (ml_dtypes.float8_e5m2, 14)}[fmt]
    v = np.moveaxis(np.asarray(x, np.float32).astype(ml_dtypes.bfloat16).astype(np.float64), axis, -1)
    blocks = v.reshape(v.shape[:-1] + (-1, 32))
    amax = np.abs(blocks).max(-1, keepdims=True)
    byte = np.maximum(np.where(amax > 0, np.frexp(amax)[1] - 1 + 127, 0) - down, 1)
    scale = np.exp2(byte - 127.0)
    codes = (blocks / scale).astype(np.float32).astype(dtype).astype(np.float64)
    return np.moveaxis((codes * scale).reshape(v.shape), -1, axis)


WIDE = False


def mx_kscale(k):
    if not WIDE:
        return np.ones(k)
    levels = np.array([10, -10, 5, -5, 0])
    if k % 512:
        return np.exp2(np.random.permutation(np.resize(levels, k // 32))).repeat(32)
    a = np.empty((k // 512, 16))
    for p in range(k // 512):
        a[p, :8] = np.random.permutation(np.resize(levels, 8))
        for g in range(8):
            far = levels[np.abs(levels - a[p, g]) >= 10]
            a[p, g + 8] = far[np.random.randint(len(far))]
    return np.exp2(a.ravel()).repeat(32)


def f64(x):
    return np.asarray(x).astype(np.float64)


def striped(idx):
    return np.tile(idx.reshape(-1, 16).T, (8, 1)).astype(np.uint16)


def unstriped(offs):
    return offs[:16].T.reshape(-1).astype(np.int64)


E2M1 = np.array([0.0, 0.5, 1.0, 1.5, 2.0, 3.0, 4.0, 6.0, -0.0, -0.5, -1.0, -1.5, -2.0, -3.0, -4.0, -6.0])


def pack_weight(w, fmt):
    k, n = w.shape
    w = f64(np.asarray(w, np.float32).astype(ml_dtypes.bfloat16)).reshape(k // 32, 32, n)
    amax = np.abs(w).max(1)
    if fmt == "e4m3":
        byte = np.frexp(amax)[1] - 1 + 127 - 7
    else:
        mant, ex = np.frexp(amax / 6.0)
        byte = np.where(mant > 0.5, ex, ex - 1) + 127
    byte = np.clip(np.where(amax > 0, byte, 1), 1, 254)
    scaled = (w * np.exp2(127.0 - byte)[:, None, :]).reshape(k, n).astype(np.float32)
    by_word = np.ascontiguousarray(scaled.reshape(k // 512, 128, 4, n).transpose(0, 1, 3, 2))
    if fmt == "e4m3":
        words = by_word.astype(ml_dtypes.float8_e4m3fn).view(np.uint8)
    else:
        c = by_word.astype(ml_dtypes.float4_e2m1fn).view(np.uint8) & 0xF
        words = (c[..., 0::2] | (c[..., 1::2] << 4)).reshape(k // 512, 128, 2 * n)
    return np.ascontiguousarray(words), np.ascontiguousarray(byte.astype(np.uint8).reshape(k // 512, 16, n))


def unpack_weight(words, scales, fmt):
    g, _, n = scales.shape
    words = np.ascontiguousarray(words).reshape(g, 128, n, -1)
    if fmt == "e4m3":
        vals = words.view(ml_dtypes.float8_e4m3fn).astype(np.float64)
    else:
        nib = np.empty((g, 128, n, 4), np.uint8)
        nib[..., 0::2] = words & 0xF
        nib[..., 1::2] = words >> 4
        vals = E2M1[nib]
    vals = vals * np.repeat(np.exp2(scales.astype(np.float64) - 127.0), 8, axis=1)[..., None]
    return vals.transpose(0, 1, 3, 2).reshape(g * 512, n)


def gelu(v):
    return 0.5 * v * (1.0 + np.tanh(np.sqrt(2.0 / np.pi) * (v + 0.044715 * v**3)))


T, S, K, H, N = 4096, 1024, 1024, 512, 768

def setup_inputs():
    n = np.random.standard_normal
    s = mx_kscale(K)[:, None]
    u = mx_kscale(H)[:, None]
    tab_words, tab_scales = pack_weight(n((K, T)) * s, "e4m3")
    w1_words, w1_scales = pack_weight(1.5 * n((K, H)) / np.sqrt(K) / s, "e2m1")
    w3_words, w3_scales = pack_weight(n((H, N)) / np.sqrt(H) / u, "e4m3")
    return {
        "tab_words": tab_words, "tab_scales": tab_scales,
        "offs": striped(np.random.permutation(T)[:S]),
        "offs2": striped(np.random.permutation(S)),
        "w1_words": w1_words, "w1_scales": w1_scales,
        "w2": (n((K, H)) / np.sqrt(K) / s).astype(np.float32),
        "gain": (np.exp(0.3 * n(H)) * u[:, 0]).astype(np.float32),
        "prior": (n((H, S)) * u).astype(np.float32),
        "w3_words": w3_words, "w3_scales": w3_scales,
        "wgo": np.exp(0.3 * n((128, S))).astype(np.float32),
        "x0": n((N, S)).astype(np.float32),
    }

def reference(tab_words, tab_scales, offs, offs2, w1_words, w1_scales, w2, gain, prior, w3_words, w3_scales, wgo, x0):
    v = unpack_weight(tab_words, tab_scales, "e4m3")[:, unstriped(offs)]
    w1 = unpack_weight(w1_words, w1_scales, "e2m1")
    g = 1.0 / (1.0 + np.exp(-(w1.T @ v)))
    e = np.tanh(mxq(f64(w2), 0, "e4m3").T @ v)
    d = g * (f64(gain)[:, None] * e - f64(prior))
    w3 = unpack_weight(w3_words, w3_scales, "e4m3")
    y = w3.T @ mxq(f64(prior), 0, "e4m3") + w3.T @ mxq(d, 0, "e4m3")
    page = np.zeros((N, S))
    page[:, unstriped(offs2)] = np.tile(f64(wgo), (N // 128, 1)) * y
    return f64(x0) - page

from contextlib import ExitStack

import concourse.mybir as mybir
from concourse.masks import make_identity

T, S, K, H, N = 4096, 1024, 1024, 512, 768
FLOPS = 2 * S * (2 * K * H + 2 * H * N)

F32 = mybir.dt.float32
BF16 = mybir.dt.bfloat16
I32 = mybir.dt.int32
U32 = mybir.dt.uint32
U16 = mybir.dt.uint16
U8 = mybir.dt.uint8
FP8X4 = mybir.dt.float8_e4m3fn_x4
FP4X4 = mybir.dt.float4_e2m1fn_x4
ACT = mybir.ActivationFunctionType
ALU = mybir.AluOpType

P = 128
PACK = 4
BANK = 512
PASSES = K // (P * PACK)
TILES = N // P
CHUNKS = ((0, 128), (128, 128), (256, 256), (512, 512))
PRIOR_LOADS = ((0, 256), (256, 256), (512, 512))


def tile_list_alert_slot_update_kernel(
    tc, tab_words, tab_scales, offs, offs2, w1_words, w1_scales, w2, gain, prior, w3_words, w3_scales, wgo, x0, out
):
    nc = tc.nc
    with ExitStack() as ctx:
        keep = ctx.enter_context(tc.tile_pool(name="keep", bufs=1))
        psum = ctx.enter_context(tc.psum_pool(name="psum", bufs=1))

        def sb(name, shape, dtype, tag=None):
            return keep.tile(shape, dtype, name=name, tag=tag or name, align_bytes=64)

        banks = [psum.tile([P, BANK], F32, name="bank%d" % b) for b in range(8)]

        idx = keep.tile([P, S // 16], U16, name="idx")
        idx2 = keep.tile([P, S // 16], U16, name="idx2")
        tab_sc = sb("tab_sc", [P, T], U8, "table_last")
        tab = [sb("tab0", [P, T], I32), sb("tab1", [P, T], I32, "table_last")]
        v = [sb("v%d" % a, [P, S], U32) for a in range(PASSES)]
        v_sc_rows = sb("v_sc_rows", [P, S], U8)
        v_sc = sb("v_sc", [P, PASSES * S], U8)
        w13 = sb("w13", [P, PACK * N], U8)
        w1_sc_raw = w13[:, 0 : PASSES * H]
        w1_raw = sb("w1_raw", [P, PASSES * 2 * H], U8)[:]
        w3 = w13[:].bitcast(I32)
        w1 = sb("w1", [P, PASSES * 2 * H], U8)
        w1_sc = sb("w1_sc", [P, PASSES * H], U8)
        w2_raw = [[sb("w2_raw%d_%d" % (a, i), [P, PACK, H // 2], F32) for i in range(2)] for a in range(PASSES)]
        w2_both = sb("w2_both", [P, 3 * PACK * H], BF16)
        w2_bf = [w2_both[:, a * PACK * H : (a + 1) * PACK * H] for a in range(PASSES)]
        w2_q = [sb("w2_q%d" % a, [P, H], U32) for a in range(PASSES)]
        w2_sc = [sb("w2_sc%d" % a, [P, H], U8) for a in range(PASSES)]
        gain_sb = sb("gain_sb", [P, PACK], F32)
        pr = [
            w2_both[:, 0 : PACK * H].bitcast(F32).rearrange("p (t j) -> p t j", t=PACK),
            w2_raw[1][1],
            w2_both[:, PACK * H : 3 * PACK * H].bitcast(F32).rearrange("p (t j) -> p t j", t=PACK),
        ]
        pr_bf = [sb("pr_bf%d" % c, [P, PACK * w], BF16) for c, (j0, w) in enumerate(CHUNKS)]
        pr_q = [sb("pr_q%d" % c, [P, w], U32) for c, (j0, w) in enumerate(CHUNKS)]
        pr_sc = [sb("pr_sc%d" % c, [P, w], U8) for c, (j0, w) in enumerate(CHUNKS)]
        gate = [sb("gate%d" % c, [P, PACK, w], F32) for c, (j0, w) in enumerate(CHUNKS)]
        e = [sb("e%d" % c, [P, PACK, w], F32) for c, (j0, w) in enumerate(CHUNKS)]
        d_bf = [sb("d_bf%d" % c, [P, PACK * w], BF16) for c, (j0, w) in enumerate(CHUNKS)]
        d_q = [sb("d_q%d" % c, [P, w], U32) for c, (j0, w) in enumerate(CHUNKS)]
        d_sc = [sb("d_sc%d" % c, [P, w], U8) for c, (j0, w) in enumerate(CHUNKS)]
        w3_sc = sb("w3_sc", [P, N], U8)
        wgo_sb = w2_raw[1][0][:].rearrange("p t j -> p (t j)")
        flat = [buf[:].rearrange("p t j -> p (t j)") for buf in (pr[0], pr[1], e[2], gate[2], e[3], gate[3])]
        x_sb = flat[0:3] + [flat[4][:, 0:S], flat[4][:, S : 2 * S], flat[5][:, S : 2 * S]]
        y_late = [flat[3][:, 0:BANK], flat[5][:, 0:BANK]]
        page = [sb("page%d" % n, [P, S], F32) for n in range(TILES)]
        y_small = [sb("y_small%d" % c, [P, 2 * P], F32) for c in range(2)]
        y_mid = sb("y_mid", [P, BANK], F32)
        y_big = [sb("y_big%d" % n, [P, BANK], F32) for n in range(TILES)]
        turned = [sb("turned%d" % i, [P, BANK], F32) for i in range(6)]
        y_third = sb("y_third", [P, 256], F32)
        ident = sb("ident", [P, P], F32)

        nc.vector.memset(tab_sc[:].bitcast(I32), 0)
        nc.gpsimd.memset(w1_sc_raw.bitcast(I32), 0)
        nc.sync.dma_start(idx[:], offs)
        nc.sync.dma_start(idx2[:], offs2)
        nc.sync.dma_start(out=gain_sb[:], in_=gain.rearrange("(p t) -> p t", t=PACK))
        w2_rows = w2.rearrange("(a p j) c -> a p j c", a=PASSES, j=PACK)
        for i in range(2):
            for j in (0, 2):
                nc.sync.dma_start(
                    out=w2_raw[0][i][:, j : j + 2, :], in_=w2_rows[0][:, j : j + 2, i * (H // 2) : (i + 1) * (H // 2)]
                )
        nc.sync.dma_start(
            out=w1_raw.bitcast(I32).rearrange("p (a c) -> p a c", a=PASSES),
            in_=w1_words.bitcast(I32).rearrange("a p c -> p a c"),
        )
        nc.sync.dma_start(
            out=tab_sc[0:P:4, :].bitcast(I32), in_=tab_scales.rearrange("a q t -> (a q) t").bitcast(I32)
        )
        for i in range(2):
            nc.sync.dma_start(out=w2_raw[1][i][:], in_=w2_rows[1][:, :, i * (H // 2) : (i + 1) * (H // 2)])
        for q in range(4):
            nc.sync.dma_start(
                out=w1_sc_raw[32 * q : 32 * q + 4, :].bitcast(I32).rearrange("p (a c) -> p a c", a=PASSES),
                in_=w1_scales.bitcast(I32)[:, 4 * q : 4 * q + 4, :].rearrange("a r c -> r a c"),
            )
        nc.sync.dma_start(out=tab[0][:], in_=tab_words[0].rearrange("p t i -> p (t i)").bitcast(I32))

        nc.vector.memset(v_sc[:].bitcast(I32), 0)
        nc.gpsimd.memset(w3_sc[:].bitcast(I32), 0)
        nc.vector.tensor_copy(v_sc_rows[:], tab_sc[:].indirect(idx[:]))
        for a in range(PASSES):
            for q in range(4):
                r0 = 64 * a + 16 * q
                nc.sync.dma_start(
                    out=v_sc[32 * q : 32 * q + 4, a * S : (a + 1) * S].bitcast(I32),
                    in_=v_sc_rows[r0 : r0 + 16 : 4, :].bitcast(I32),
                )
            if a == 0:
                nc.sync.dma_start(out=tab[1][:], in_=tab_words[1].rearrange("p t i -> p (t i)").bitcast(I32))

        for q in range(4):
            nc.gpsimd.dma_start(
                out=w3_sc[32 * q : 32 * q + 4, :].bitcast(I32), in_=w3_scales.bitcast(I32)[0, 4 * q : 4 * q + 4, :]
            )
        make_identity(nc, ident[:])

        nc.vector.tensor_copy(
            out=w1[:].bitcast(U16).rearrange("p (a t m) -> p a m t", a=PASSES, t=PACK),
            in_=w1_raw.bitcast(U16).rearrange("p (a m t) -> p a m t", a=PASSES, t=PACK),
        )
        nc.vector.tensor_copy(
            out=w1_sc[:].rearrange("p (a t m) -> p a m t", a=PASSES, t=PACK),
            in_=w1_sc_raw.rearrange("p (a m t) -> p a m t", a=PASSES, t=PACK),
        )

        def w2_round(a, i):
            nc.scalar.copy(
                out=w2_bf[a][:].rearrange("p (t m j) -> p m j t", t=PACK, j=PACK)[:, i * 64 : (i + 1) * 64],
                in_=w2_raw[a][i][:].rearrange("p j (m t) -> p m j t", t=PACK),
            )

        def load_prior(i):
            j0, w = PRIOR_LOADS[i]
            nc.sync.dma_start(out=pr[i][:], in_=prior.rearrange("(p t) j -> p t j", t=PACK)[:, :, j0 : j0 + w])

        def load_x(n):
            nc.sync.dma_start(out=x_sb[n], in_=x0[n * P : (n + 1) * P, :])

        def quantize(codes, scales, values):
            nc.vector.quantize_mx(out=codes[:].bitcast(FP8X4), scales=scales[:], in_=values[:])

        def first_passes(c, weights, bank_ids, b0, passes):
            j0, w = CHUNKS[c]
            per_bank = BANK // w
            width = BANK if w == BANK else P
            for a in passes:
                for b, bank in enumerate(bank_ids):
                    for i in range(BANK // width):
                        t = (b0 + b) * per_bank + i * width // w
                        jj = j0 + i * width % w
                        codes, scales = weights(a, t)
                        nc.tensor.matmul_mx(
                            out=banks[bank][:, i * width : (i + 1) * width],
                            lhsT=codes,
                            lhsT_scale=scales,
                            rhs=v[a][:, jj : jj + width].bitcast(FP8X4),
                            rhs_scale=v_sc[:, a * S + jj : a * S + jj + width],
                            start=(a == 0 and i == 0),
                            stop=(a == PASSES - 1 and i == BANK // width - 1),
                        )

        def first_stage(c, weights, func, dest, bank_ids, passes):
            per_bank = BANK // CHUNKS[c][1]
            for b0 in range(0, PACK // per_bank, len(bank_ids)):
                first_passes(c, weights, bank_ids, b0, passes)
                for b, bank in enumerate(bank_ids):
                    t0 = (b0 + b) * per_bank
                    nc.scalar.activation(
                        out=dest[c][:, t0 : t0 + per_bank, :].rearrange("p t j -> p (t j)"), in_=banks[bank][:], func=func
                    )

        def w1_slice(a, t):
            c0 = a * H + t * P
            return w1[:, 2 * c0 : 2 * (c0 + P)].bitcast(FP4X4), w1_sc[:, c0 : c0 + P]

        def w2_slice(a, t):
            return w2_q[a][:, t * P : (t + 1) * P].bitcast(FP8X4), w2_sc[a][:, t * P : (t + 1) * P]

        def suggestion(c, bank_ids, passes):
            first_stage(c, w2_slice, ACT.Tanh, e, bank_ids, passes)

        def gating(c, bank_ids, passes):
            first_stage(c, w1_slice, ACT.Sigmoid, gate, bank_ids, passes)

        def prior_round(c):
            i, cols = prior_part(c)
            nc.scalar.copy(
                out=pr_bf[c][:].rearrange("p (c i t) -> p c t i", t=PACK, i=4),
                in_=pr[i][:, :, cols].rearrange("p t (c i) -> p c t i", i=4),
            )

        def prior_part(c):
            j0, w = CHUNKS[c]
            for i, (l0, lw) in enumerate(PRIOR_LOADS):
                if l0 <= j0 < l0 + lw:
                    return i, slice(j0 - l0, j0 - l0 + w)

        def shift(c):
            j0, w = CHUNKS[c]
            i, cols = prior_part(c)
            for t in range(PACK):
                nc.vector.scalar_tensor_tensor(
                    out=e[c][:, t, :],
                    in0=e[c][:, t, :],
                    scalar=gain_sb[:, t : t + 1],
                    in1=pr[i][:, t, cols],
                    op0=ALU.mult,
                    op1=ALU.subtract,
                )
            nc.vector.tensor_tensor(
                out=d_bf[c][:].rearrange("p (c i t) -> p c t i", t=PACK, i=4),
                in0=e[c][:].rearrange("p t (c i) -> p c t i", i=4),
                in1=gate[c][:].rearrange("p t (c i) -> p c t i", i=4),
                op=ALU.mult,
            )

        def product(c, tiles, bank):
            j0, w = CHUNKS[c]
            sides = ((pr_q[c][:], pr_sc[c][:]), (d_q[c][:], d_sc[c][:]))
            for s, (codes, scales) in enumerate(sides):
                for k, n in enumerate(tiles):
                    nc.tensor.matmul_mx(
                        out=banks[bank][:, k * w : (k + 1) * w],
                        lhsT=w3[:, n * P : (n + 1) * P].bitcast(FP8X4),
                        lhsT_scale=w3_sc[:, n * P : (n + 1) * P],
                        rhs=codes.bitcast(FP8X4),
                        rhs_scale=scales,
                        start=(s == 0 and k == 0),
                        stop=(s == 1 and k == len(tiles) - 1),
                    )

        def negated(dest, src):
            nc.scalar.activation(out=dest, in_=src, func=ACT.Copy, scale=-1.0)

        def scatter(c, n, src):
            j0, w = CHUNKS[c]
            nc.vector.tensor_tensor(
                page[n][:].indirect(idx2[:, j0 // 16 : (j0 + w) // 16]), src, wgo_sb[:, j0 : j0 + w], ALU.mult
            )

        def small_chunk(c, tiles, bank, dest):
            w = CHUNKS[c][1]
            product(c, tiles, bank)
            negated(dest, banks[bank][:, 0 : len(tiles) * w])
            for i, n in enumerate(tiles):
                scatter(c, n, dest[:, i * w : (i + 1) * w])

        def finish_on_tensor(n):
            pair = 2 * (n % 3)
            first, second = ((4, 5), (6, 7)) if n % 2 == 0 else ((6, 7), (4, 5))
            for h in range(2):
                for s, src in enumerate((x_sb[n], page[n])):
                    for k in range(4):
                        m0 = h * BANK + k * P
                        nc.tensor.matmul(
                            out=banks[first[h]][:, k * P : (k + 1) * P],
                            lhsT=src[:, m0 : m0 + P],
                            rhs=ident[:],
                            is_transpose=True,
                            start=(s == 0 and k == 0),
                            stop=(s == 1 and k == 3),
                        )
                nc.scalar.copy(out=turned[pair + h][:], in_=banks[first[h]][:])
            for h in range(2):
                for k in range(4):
                    nc.tensor.transpose(
                        banks[second[h]][:, k * P : (k + 1) * P], turned[pair + h][:, k * P : (k + 1) * P], ident[:]
                    )
                cols = slice(h * BANK, (h + 1) * BANK)
                nc.scalar.copy(out=x_sb[n][:, cols], in_=banks[second[h]][:])
                nc.sync.dma_start(out=out[n * P : (n + 1) * P, cols], in_=x_sb[n][:, cols])

        def finish_on_vector(n):
            for h in range(2):
                cols = slice(h * BANK, (h + 1) * BANK)
                nc.vector.tensor_tensor(x_sb[n][:, cols], x_sb[n][:, cols], page[n][:, cols], ALU.add)
                nc.sync.dma_start(out=out[n * P : (n + 1) * P, cols], in_=x_sb[n][:, cols])

        warm = sb("warm", [P, 8], F32)
        nc.vector.memset(warm[:], 0.0)
        nc.scalar.activation(out=warm[:], in_=warm[:], func=ACT.Sigmoid)
        for a in range(PASSES):
            for i in range(2):
                w2_round(a, i)
            quantize(w2_q[a], w2_sc[a], w2_bf[a])
        load_prior(0)
        nc.sync.dma_start(out=w3, in_=w3_words[0].rearrange("p c i -> p (c i)").bitcast(I32))
        nc.sync.dma_start(out=wgo_sb, in_=wgo)
        load_prior(1)
        load_prior(2)
        nc.vector.tensor_copy(v[0][:], tab[0][:].bitcast(U32).indirect(idx[:]))
        for c, (e_banks, g_banks) in enumerate((((0,), (1,)), ((2,), (3,)), ((4, 5), (6, 7)))):
            first_passes(c, w2_slice, e_banks, 0, (0,))
            first_passes(c, w1_slice, g_banks, 0, (0,))
        for h in range(2):
            nc.vector.tensor_copy(
                v[1][:, h * BANK : (h + 1) * BANK], tab[1][:].bitcast(U32).indirect(idx[:, h * 32 : (h + 1) * 32])
            )
        prior_round(0)
        suggestion(0, (0,), (1,))
        gating(0, (1,), (1,))
        shift(0)
        quantize(pr_q[0], pr_sc[0], pr_bf[0])
        quantize(d_q[0], d_sc[0], d_bf[0])
        suggestion(1, (2,), (1,))
        gating(1, (3,), (1,))
        prior_round(1)
        shift(1)
        quantize(pr_q[1], pr_sc[1], pr_bf[1])
        quantize(d_q[1], d_sc[1], d_bf[1])
        load_x(0)
        small_chunk(0, (0, 1), 0, y_small[0][:])
        small_chunk(1, (0, 1), 2, y_small[1][:])
        suggestion(2, (4, 5), (1,))
        gating(2, (6, 7), (1,))
        prior_round(2)
        shift(2)
        quantize(pr_q[2], pr_sc[2], pr_bf[2])
        quantize(d_q[2], d_sc[2], d_bf[2])
        for n in (1, 2):
            load_x(n)
        small_chunk(0, (2, 3, 4, 5), 1, y_late[0])
        small_chunk(2, (0, 1), 0, y_mid[:])
        product(2, (2, 3), 2)
        negated(y_third[:], banks[2][:, 0:256])
        product(2, (4, 5), 0)
        suggestion(3, (4, 5), (0, 1))
        gating(3, (6, 7), (0, 1))
        prior_round(3)
        shift(3)
        quantize(pr_q[3], pr_sc[3], pr_bf[3])
        quantize(d_q[3], d_sc[3], d_bf[3])
        for n in (3, 4, 5):
            load_x(n)
        small_chunk(1, (2, 3, 4, 5), 3, y_late[1])
        for n, bank in enumerate((1, 4, 5, 6, 7, 3)):
            product(3, (n,), bank)
            negated(y_big[n][:], banks[bank][:])
        y_next = [y_third[:]] + [turned[2 * n + 1][:, 0:256] for n in range(3)]
        for n in range(TILES):
            if n >= 2:
                scatter(2, n, y_next[n - 2])
            scatter(3, n, y_big[n][:])
            if n < TILES - 1:
                finish_on_tensor(n)
            else:
                finish_on_vector(n)
            if n < 3:
                m = n + 3
                negated(y_next[m - 2], banks[2 if m < 4 else 0][:, (m % 2) * 256 : (m % 2 + 1) * 256])
